import numpy as np
CORES = [3,5,19,21,35,37,51,53,67,69]
N = 10
CB = 64
def setup_inputs(rng):
    return {"x": rng.standard_normal((N, 128, N * CB), dtype=np.float32)}
def setup_inputs_big(rng):
    d = setup_inputs(rng)
    for k in ("x",): d[k] = (d[k].astype(np.float32) * 1024.0).astype(d[k].dtype)
    return d
def setup_inputs_small(rng):
    d = setup_inputs(rng)
    for k in ("x",): d[k] = (d[k].astype(np.float32) * (1 / 1024.0)).astype(d[k].dtype)
    return d
def setup_inputs_apart(rng):
    d = setup_inputs(rng)
    f = (10.0 ** rng.permutation(np.linspace(-1.5, 1.5, N))).astype(np.float32).reshape(N, 1, 1)
    for k in ("x",): d[k] = (d[k].astype(np.float32) * f).astype(d[k].dtype)
    return d
def reference(x):
    X = x.astype(np.float64)
    G = sum(X[j].T @ X[j] for j in range(N))
    y = np.full((N, CB, N * CB), np.nan)
    for r in range(N):
        y[r][:, :CB * r] = G[CB * r:CB * r + CB, :CB * r]
    return {"y": y.astype(np.float32 if x.dtype != np.float64 else np.float64)}

@@ -1,0 +1,192 @@
+from concourse.mybir import AluOpType
+
+N = 10
+CB = 64
+P = 128
+NCH = 5
+WMAX = 32 * (N - 1)
+
+JOBS = {
+    0: ((1, 4), (3, 2)),
+    1: ((3, 2), (4, 0)),
+    2: ((4, 0), (1, 3)),
+    3: ((2, 1, 0), (4,)),
+    4: ((3, 0), (2, 1)),
+}
+NSEND = 6
+NBANK = 5
+
+SCRATCH = {
+    "xa": ("sbuf", [P, N * CB], "float32"),
+    "xb": ("sbuf", [P, N * CB], "float32"),
+    "lz": ("sbuf", [P, 2 * CB], "float32"),
+    "res": ("sbuf", [P, WMAX], "float32"),
+}
+for _k in range(NCH):
+    SCRATCH["land%d" % _k] = ("sbuf", [P, WMAX], "float32")
+for _k in range(NSEND):
+    SCRATCH["stage%d" % _k] = ("sbuf", [P, WMAX], "float32")
+for _k in range(NBANK):
+    SCRATCH["ps%d" % _k] = ("psum", [P, 512], "float32")
+
+SEMAPHORES = (["ld", "lzs", "xr", "snt", "ad", "fin", "st"]
+              + ["pe%d" % i for i in range(NBANK)]
+              + ["ar%d" % i for i in range(NCH)]
+              + ["cp%d" % i for i in range(NSEND)])
+
+
+def _count(mask):
+    return bin(mask).count("1")
+
+
+def rank_program(g, core, T, topo):
+    rank = T.rank_of(core)
+    if rank is None:
+        return
+    S = T.sem
+    cores = list(T.cores)
+    chips = []
+    for c in cores:
+        if topo.chip(c) not in chips:
+            chips.append(topo.chip(c))
+
+    def chip_index(c):
+        return chips.index(topo.chip(c))
+
+    def side_of(c):
+        return 0 if topo.die(c) == topo.die(cores[0]) else 1
+
+    def member(k, side):
+        return [c for c in cores if chip_index(c) == k and side_of(c) == side][0]
+
+    def sender(k, d):
+        return member(k, 0 if d in JOBS[k][0] else 1)
+
+    def jobs_of(c):
+        return JOBS[chip_index(c)][side_of(c)]
+
+    def columns_read(c):
+        top = [P * d + P for d in jobs_of(c)] + [CB * T.rank_of(c) + CB]
+        return max(top)
+
+    def units_before(k, r):
+        u = 0
+        for d in jobs_of(sender(k, r // 2)):
+            for q in (2 * d + 1, 2 * d):
+                u += q
+                if q == r:
+                    return u
+        return u
+
+    me = chip_index(core)
+    partner = member(me, 1 - side_of(core))
+    jobs = jobs_of(core)
+    sent = [0]
+
+    def send(dst, out_ap, in_ap, sem):
+        rid, pid, _se = topo.addr(dst)
+        m = topo.mask(core, dst)
+        g.remote_dma(out_ap=out_ap, in_ap=in_ap, remote_sem=sem, local_sem=S.snt, pid=pid, routing_id=rid,
+                     dma_engine_mask=m)
+        sent[0] += _count(m)
+
+    nb = 0
+    seg = {}
+    for d in jobs:
+        nc = P * d + CB
+        cuts = [0, nc] if nc <= 512 else [0, nc // 2, nc]
+        seg[d] = []
+        for i in range(len(cuts) - 1):
+            seg[d].append((nb, cuts[i], cuts[i + 1]))
+            nb += 1
+    own_bank = nb
+    w_own = 32 * rank
+
+    g.sync.dma_start(T.xa[:, :], T.x[:, :]).then_inc(S.ld, 16)
+
+    need = columns_read(partner)
+    g.wait_ge(S.ld, 16)
+    send(partner, T.xb[:, 0:need], T.xa[:, 0:need], S.xr)
+
+    if rank > 0:
+        g.vector.memset(T.lz[:, CB:2 * CB], 0.0).then_inc(S.lzs, 1)
+        g.vector.wait_ge(S.ld, 16)
+        g.vector.tensor_copy(T.lz[:, 0:CB], T.xa[:, CB * rank:CB * rank + CB]).then_inc(S.lzs, 1)
+
+    def job_pass(xs, first):
+        for d in jobs:
+            for (b, lo, hi) in seg[d]:
+                ins = g.tensor.matmul(T["ps%d" % b][:, 0:hi - lo], xs[:, P * d:P * d + P], xs[:, lo:hi],
+                                      first, not first)
+                if not first:
+                    ins.then_inc(S["pe%d" % b], 1)
+
+    def own_pass(xs, first):
+        ps = T["ps%d" % own_bank]
+        w = w_own
+        blk = xs[:, CB * rank:CB * rank + CB]
+        if first:
+            g.tensor.matmul(ps[:, 0:w], T.lz[:, :], xs[:, 0:w], True, False)
+            g.tensor.matmul(ps[64:128, 0:w], blk, xs[:, w:2 * w], False, False)
+        else:
+            g.tensor.matmul(ps[0:64, 0:w], blk, xs[:, 0:w], False, True).then_inc(S["pe%d" % own_bank], 1)
+            g.tensor.matmul(ps[64:128, 0:w], blk, xs[:, w:2 * w], False, True).then_inc(S["pe%d" % own_bank], 1)
+
+    g.tensor.wait_ge(S.ld, 16)
+    job_pass(T.xa, True)
+    if rank > 0:
+        g.tensor.wait_ge(S.lzs, 2)
+        own_pass(T.xa, True)
+    g.tensor.wait_ge(S.xr, _count(topo.mask(partner, core)))
+    job_pass(T.xb, False)
+    if rank > 0:
+        own_pass(T.xb, False)
+
+    n = 0
+    seen = []
+    for d in jobs:
+        for r in (2 * d + 1, 2 * d):
+            if r == 0:
+                continue
+            w = 32 * r
+            p0 = CB * (r - 2 * d)
+            st = T["stage%d" % n]
+            cnt = 0
+            for h in (0, 1):
+                for (b, lo, hi) in seg[d]:
+                    a = max(lo, h * w)
+                    e = min(hi, (h + 1) * w)
+                    if a >= e:
+                        continue
+                    if b not in seen:
+                        g.vector.wait_ge(S["pe%d" % b], 1)
+                        seen.append(b)
+                    g.vector.tensor_copy(st[CB * h:CB * h + CB, a - h * w:e - h * w],
+                                         T["ps%d" % b][p0:p0 + CB, a - lo:e - lo]).then_inc(S["cp%d" % n], 1)
+                    cnt += 1
+            g.wait_ge(S["cp%d" % n], cnt)
+            send(cores[r], T["land%d" % me][:, 0:w], st[:, 0:w], S["ar%d" % me])
+            n += 1
+
+    if rank > 0:
+        w = w_own
+        ps = T["ps%d" % own_bank]
+        g.vector.wait_ge(S["pe%d" % own_bank], 2)
+        srcs = [k for k in range(NCH) if k != me]
+        srcs.sort(key=lambda k: units_before(k, rank))
+        for j, k in enumerate(srcs):
+            g.vector.wait_ge(S["ar%d" % k], _count(topo.mask(sender(k, me), core)))
+            if j:
+                g.vector.wait_ge(S.ad, j)
+            if j == len(srcs) - 1:
+                g.vector.tensor_tensor(T.res[:, 0:w], ps[:, 0:w], T["land%d" % k][:, 0:w],
+                                       AluOpType.add).then_inc(S.fin, 1)
+            else:
+                g.vector.tensor_tensor(ps[:, 0:w], ps[:, 0:w], T["land%d" % k][:, 0:w],
+                                       AluOpType.add).then_inc(S.ad, 1)
+        g.sync.wait_ge(S.fin, 1)
+        g.scalar.wait_ge(S.fin, 1)
+        g.sync.dma_start(T.y[:, 0:w], T.res[0:64, 0:w]).then_inc(S.st, 16)
+        g.scalar.dma_start(T.y[:, w:2 * w], T.res[64:128, 0:w]).then_inc(S.st, 16)
+        g.wait_ge(S.st, 32)
+    g.wait_ge(S.snt, sent[0])

@@ -7,14 +7,16 @@ NCH = 5
 WMAX = 32 * (N - 1)
 
 JOBS = {
-    0: ((1, 4), (3, 2)),
+    0: ((4, 1), (3, 2)),
     1: ((3, 2), (4, 0)),
-    2: ((4, 0), (1, 3)),
+    2: ((4, 0), (3, 1)),
     3: ((2, 1, 0), (4,)),
     4: ((3, 0), (2, 1)),
 }
+EARLY = {9: 128}
+EMAX = max(EARLY.values())
 NSEND = 6
-NBANK = 5
+NBANK = 8
 
 SCRATCH = {
     "xa": ("sbuf", [P, N * CB], "float32"),
@@ -24,6 +26,10 @@ SCRATCH = {
 }
 for _k in range(NCH):
     SCRATCH["land%d" % _k] = ("sbuf", [P, WMAX], "float32")
+for _k in range(N):
+    SCRATCH["el%d" % _k] = ("sbuf", [P, EMAX], "float32")
+for _k in range(len(EARLY)):
+    SCRATCH["es%d" % _k] = ("sbuf", [P, EMAX], "float32")
 for _k in range(NSEND):
     SCRATCH["stage%d" % _k] = ("sbuf", [P, WMAX], "float32")
 for _k in range(NBANK):
@@ -32,6 +38,8 @@ for _k in range(NBANK):
 SEMAPHORES = (["ld", "lzs", "xr", "snt", "ad", "fin", "st"]
               + ["pe%d" % i for i in range(NBANK)]
               + ["ar%d" % i for i in range(NCH)]
+              + ["ea%d" % i for i in range(N)]
+              + ["ec%d" % i for i in range(len(EARLY))]
               + ["cp%d" % i for i in range(NSEND)])
 
 
@@ -81,6 +89,7 @@ def rank_program(g, core, T, topo):
     me = chip_index(core)
     partner = member(me, 1 - side_of(core))
     jobs = jobs_of(core)
+    early = [r for r in sorted(EARLY, reverse=True) if chip_index(cores[r]) != me]
     sent = [0]
 
     def send(dst, out_ap, in_ap, sem):
@@ -100,6 +109,7 @@ def rank_program(g, core, T, topo):
             seg[d].append((nb, cuts[i], cuts[i + 1]))
             nb += 1
     own_bank = nb
+    nb += 1
     w_own = 32 * rank
 
     g.sync.dma_start(T.xa[:, :], T.x[:, :]).then_inc(S.ld, 16)
@@ -107,6 +117,20 @@ def rank_program(g, core, T, topo):
     need = columns_read(partner)
     g.wait_ge(S.ld, 16)
     send(partner, T.xb[:, 0:need], T.xa[:, 0:need], S.xr)
+
+    g.tensor.wait_ge(S.ld, 16)
+    for i, r in enumerate(early):
+        e = EARLY[r]
+        w = 32 * r
+        ps = T["ps%d" % (nb + i)]
+        pe = S["pe%d" % (nb + i)]
+        blk = T.xa[:, CB * r:CB * r + CB]
+        g.tensor.matmul(ps[0:64, 0:e], blk, T.xa[:, 0:e], True, True).then_inc(pe, 1)
+        g.tensor.matmul(ps[64:128, 0:e], blk, T.xa[:, w:w + e], True, True).then_inc(pe, 1)
+        g.vector.wait_ge(pe, 2)
+        g.vector.tensor_copy(T["es%d" % i][:, 0:e], ps[:, 0:e]).then_inc(S["ec%d" % i], 1)
+        g.wait_ge(S["ec%d" % i], 1)
+        send(cores[r], T["el%d" % rank][:, 0:e], T["es%d" % i][:, 0:e], S["ea%d" % rank])
 
     if rank > 0:
         g.vector.memset(T.lz[:, CB:2 * CB], 0.0).then_inc(S.lzs, 1)
@@ -132,7 +156,6 @@ def rank_program(g, core, T, topo):
             g.tensor.matmul(ps[0:64, 0:w], blk, xs[:, 0:w], False, True).then_inc(S["pe%d" % own_bank], 1)
             g.tensor.matmul(ps[64:128, 0:w], blk, xs[:, w:2 * w], False, True).then_inc(S["pe%d" % own_bank], 1)
 
-    g.tensor.wait_ge(S.ld, 16)
     job_pass(T.xa, True)
     if rank > 0:
         g.tensor.wait_ge(S.lzs, 2)
@@ -148,13 +171,14 @@ def rank_program(g, core, T, topo):
         for r in (2 * d + 1, 2 * d):
             if r == 0:
                 continue
+            e0 = EARLY.get(r, 0)
             w = 32 * r
             p0 = CB * (r - 2 * d)
             st = T["stage%d" % n]
             cnt = 0
             for h in (0, 1):
                 for (b, lo, hi) in seg[d]:
-                    a = max(lo, h * w)
+                    a = max(lo, h * w + e0)
                     e = min(hi, (h + 1) * w)
                     if a >= e:
                         continue
@@ -165,27 +189,35 @@ def rank_program(g, core, T, topo):
                                          T["ps%d" % b][p0:p0 + CB, a - lo:e - lo]).then_inc(S["cp%d" % n], 1)
                     cnt += 1
             g.wait_ge(S["cp%d" % n], cnt)
-            send(cores[r], T["land%d" % me][:, 0:w], st[:, 0:w], S["ar%d" % me])
+            send(cores[r], T["land%d" % me][:, e0:w], st[:, e0:w], S["ar%d" % me])
             n += 1
 
     if rank > 0:
         w = w_own
+        e0 = EARLY.get(rank, 0)
         ps = T["ps%d" % own_bank]
         g.vector.wait_ge(S["pe%d" % own_bank], 2)
+        parts = []
+        if e0:
+            parts.append((0, e0, [(T["el%d" % q], S["ea%d" % q], _count(topo.mask(cores[q], core)))
+                                  for q in range(N) if chip_index(cores[q]) != me]))
         srcs = [k for k in range(NCH) if k != me]
         srcs.sort(key=lambda k: units_before(k, rank))
-        for j, k in enumerate(srcs):
-            g.vector.wait_ge(S["ar%d" % k], _count(topo.mask(sender(k, me), core)))
-            if j:
-                g.vector.wait_ge(S.ad, j)
-            if j == len(srcs) - 1:
-                g.vector.tensor_tensor(T.res[:, 0:w], ps[:, 0:w], T["land%d" % k][:, 0:w],
-                                       AluOpType.add).then_inc(S.fin, 1)
-            else:
-                g.vector.tensor_tensor(ps[:, 0:w], ps[:, 0:w], T["land%d" % k][:, 0:w],
-                                       AluOpType.add).then_inc(S.ad, 1)
-        g.sync.wait_ge(S.fin, 1)
-        g.scalar.wait_ge(S.fin, 1)
+        parts.append((e0, w, [(T["land%d" % k], S["ar%d" % k], _count(topo.mask(sender(k, me), core)))
+                              for k in srcs]))
+        nad = 0
+        for (a, b, lands) in parts:
+            for j, (buf, sem, cnt) in enumerate(lands):
+                g.vector.wait_ge(sem, cnt)
+                if nad:
+                    g.vector.wait_ge(S.ad, nad)
+                if j == len(lands) - 1:
+                    g.vector.tensor_tensor(T.res[:, a:b], ps[:, a:b], buf[:, a:b], AluOpType.add).then_inc(S.fin, 1)
+                else:
+                    g.vector.tensor_tensor(ps[:, a:b], ps[:, a:b], buf[:, a:b], AluOpType.add).then_inc(S.ad, 1)
+                    nad += 1
+        g.sync.wait_ge(S.fin, len(parts))
+        g.scalar.wait_ge(S.fin, len(parts))
         g.sync.dma_start(T.y[:, 0:w], T.res[0:64, 0:w]).then_inc(S.st, 16)
         g.scalar.dma_start(T.y[:, w:2 * w], T.res[64:128, 0:w]).then_inc(S.st, 16)
         g.wait_ge(S.st, 32)

@@ -4,7 +4,12 @@ N = 10
 CB = 64
 P = 128
 NCH = 5
+TOP = NCH - 1
 WMAX = 32 * (N - 1)
+EC = 128
+CUT = 320
+NSEND = 8
+NBANK = 8
 
 JOBS = {
     0: ((4, 1), (3, 2)),
@@ -13,33 +18,102 @@ JOBS = {
     3: ((2, 1, 0), (4,)),
     4: ((3, 0), (2, 1)),
 }
-EARLY = {9: 128}
-EMAX = max(EARLY.values())
-NSEND = 6
-NBANK = 8
+OWN_LAST = ((1, 0),)
+
+
+def _w(d):
+    return P * d + CB
+
+
+def _unit(k, d, lo, hi):
+    if d == TOP and k != TOP:
+        return (TOP, 0, EC) if hi <= EC else (TOP, EC, _w(TOP))
+    return (d, 0, _w(d))
+
+
+def _segs(k, d):
+    lo = EC if (d == TOP and k != TOP) else 0
+    if P * d >= CUT and _w(d) > CUT:
+        return [(d, CUT, _w(d)), (d, lo, CUT)]
+    return [(d, lo, _w(d))]
+
+
+def _plan(k, side):
+    jobs = JOBS[k][side]
+    first = _segs(k, jobs[0])
+    own = _segs(k, k)
+    ahead, rest = [], []
+    if k == TOP:
+        ahead += [("R",) + own[0]]
+        rest += [("R",) + s for s in own[1:]]
+        own = []
+    if len(first) > 1:
+        ahead += [("C1",) + first[0]]
+        rest += [("C1",) + first[1]]
+    else:
+        rest += [("C1",) + first[0]]
+    prog = list(ahead)
+    if k != TOP:
+        prog += [("R", TOP, 0, EC)]
+    prog += rest
+    if (k, side) not in OWN_LAST:
+        prog += [("R",) + s for s in own]
+    for d in jobs[1:]:
+        prog += [("C1",) + s for s in _segs(k, d)]
+    for d in jobs:
+        prog += [("C2",) + s for s in _segs(k, d)]
+    if (k, side) in OWN_LAST:
+        prog += [("R",) + s for s in own]
+    return prog
+
+
+def _parts(r):
+    w = CB * r
+    if r // 2 == TOP:
+        return [(0, EC, 0, EC // 2), (EC, w, EC // 2, (w - EC) // 2)]
+    return [(0, w, 0, w // 2)]
+
+
+def _lrange(r, unit):
+    _d, lo, hi = unit
+    sel = [(off, off + wp) for (c0, c1, off, wp) in _parts(r) if c0 < hi and c1 > lo]
+    return min(a for a, _b in sel), max(b for _a, b in sel)
+
+
+def _finished(k, prog):
+    left = {}
+    for (kind, d, lo, hi) in prog:
+        if kind != "C1":
+            u = _unit(k, d, lo, hi)
+            left[u] = left.get(u, 0) + 1
+    out = []
+    col = 0
+    for (kind, d, lo, hi) in prog:
+        col += hi - lo
+        if kind != "C1":
+            u = _unit(k, d, lo, hi)
+            left[u] -= 1
+            if left[u] == 0:
+                out.append((u, col))
+    return out
+
 
 SCRATCH = {
     "xa": ("sbuf", [P, N * CB], "float32"),
     "xb": ("sbuf", [P, N * CB], "float32"),
-    "lz": ("sbuf", [P, 2 * CB], "float32"),
     "res": ("sbuf", [P, WMAX], "float32"),
 }
-for _k in range(NCH):
-    SCRATCH["land%d" % _k] = ("sbuf", [P, WMAX], "float32")
 for _k in range(N):
-    SCRATCH["el%d" % _k] = ("sbuf", [P, EMAX], "float32")
-for _k in range(len(EARLY)):
-    SCRATCH["es%d" % _k] = ("sbuf", [P, EMAX], "float32")
+    SCRATCH["land%d" % _k] = ("sbuf", [P, WMAX], "float32")
 for _k in range(NSEND):
     SCRATCH["stage%d" % _k] = ("sbuf", [P, WMAX], "float32")
 for _k in range(NBANK):
     SCRATCH["ps%d" % _k] = ("psum", [P, 512], "float32")
 
-SEMAPHORES = (["ld", "lzs", "xr", "snt", "ad", "fin", "st"]
+SEMAPHORES = (["ldr", "ldl", "xrr", "xrl", "snt", "ad", "fin0", "fin1", "st"]
               + ["pe%d" % i for i in range(NBANK)]
-              + ["ar%d" % i for i in range(NCH)]
+              + ["ar%d" % i for i in range(N)]
               + ["ea%d" % i for i in range(N)]
-              + ["ec%d" % i for i in range(len(EARLY))]
               + ["cp%d" % i for i in range(NSEND)])
 
 
@@ -67,158 +141,145 @@ def rank_program(g, core, T, topo):
     def member(k, side):
         return [c for c in cores if chip_index(c) == k and side_of(c) == side][0]
 
-    def sender(k, d):
-        return member(k, 0 if d in JOBS[k][0] else 1)
+    def tile_mask(src, dst):
+        m = topo.mask(src, dst)
+        if topo.chip(src) != topo.chip(dst):
+            return m
+        far = [c for c in cores if topo.chip(c) != topo.chip(src)][0]
+        rest = m & ~topo.mask(src, far)
+        return rest if rest and P % _count(rest) == 0 else m
 
-    def jobs_of(c):
-        return JOBS[chip_index(c)][side_of(c)]
-
-    def columns_read(c):
-        top = [P * d + P for d in jobs_of(c)] + [CB * T.rank_of(c) + CB]
-        return max(top)
-
-    def units_before(k, r):
-        u = 0
-        for d in jobs_of(sender(k, r // 2)):
-            for q in (2 * d + 1, 2 * d):
-                u += q
-                if q == r:
-                    return u
-        return u
+    def sends_of(c):
+        rq = T.rank_of(c)
+        k = chip_index(c)
+        out = []
+        for (u, col) in _finished(k, _plan(k, side_of(c))):
+            d = u[0]
+            for r in (2 * d + 1, 2 * d):
+                if r == 0 or r == rq:
+                    continue
+                a, b = _lrange(r, u)
+                out.append((r, u, a, b, ("ea%d" if u == (TOP, 0, EC) else "ar%d") % rq, col))
+        return out
 
     me = chip_index(core)
     partner = member(me, 1 - side_of(core))
-    jobs = jobs_of(core)
-    early = [r for r in sorted(EARLY, reverse=True) if chip_index(cores[r]) != me]
+    prog = _plan(me, side_of(core))
     sent = [0]
 
-    def send(dst, out_ap, in_ap, sem):
+    def send(dst, out_ap, in_ap, sem, m):
         rid, pid, _se = topo.addr(dst)
-        m = topo.mask(core, dst)
         g.remote_dma(out_ap=out_ap, in_ap=in_ap, remote_sem=sem, local_sem=S.snt, pid=pid, routing_id=rid,
                      dma_engine_mask=m)
         sent[0] += _count(m)
 
     nb = 0
+    bank = {}
     seg = {}
-    for d in jobs:
-        nc = P * d + CB
-        cuts = [0, nc] if nc <= 512 else [0, nc // 2, nc]
-        seg[d] = []
-        for i in range(len(cuts) - 1):
-            seg[d].append((nb, cuts[i], cuts[i + 1]))
-            nb += 1
-    own_bank = nb
-    nb += 1
-    w_own = 32 * rank
+    for (_kind, d, lo, hi) in prog:
+        if (d, lo, hi) in bank:
+            continue
+        bank[(d, lo, hi)] = nb
+        seg.setdefault(_unit(me, d, lo, hi), []).append((nb, lo, hi))
+        nb += 1
+    acc = T["ps%d" % nb]
 
-    g.sync.dma_start(T.xa[:, :], T.x[:, :]).then_inc(S.ld, 16)
+    g.sync.dma_start(T.xa[:, CUT:N * CB], T.x[:, CUT:N * CB]).then_inc(S.ldr, 16)
+    g.sync.dma_start(T.xa[:, 0:CUT], T.x[:, 0:CUT]).then_inc(S.ldl, 16)
 
-    need = columns_read(partner)
-    g.wait_ge(S.ld, 16)
-    send(partner, T.xb[:, 0:need], T.xa[:, 0:need], S.xr)
+    need = max(max(P * d + P, hi) for (kind, d, lo, hi) in _plan(me, 1 - side_of(core)) if kind == "C2")
+    g.wait_ge(S.ldr, 16)
+    send(partner, T.xb[:, CUT:need], T.xa[:, CUT:need], S.xrr, topo.mask(core, partner))
+    g.wait_ge(S.ldl, 16)
+    send(partner, T.xb[:, 0:CUT], T.xa[:, 0:CUT], S.xrl, topo.mask(core, partner))
 
-    g.tensor.wait_ge(S.ld, 16)
-    for i, r in enumerate(early):
-        e = EARLY[r]
-        w = 32 * r
-        ps = T["ps%d" % (nb + i)]
-        pe = S["pe%d" % (nb + i)]
-        blk = T.xa[:, CB * r:CB * r + CB]
-        g.tensor.matmul(ps[0:64, 0:e], blk, T.xa[:, 0:e], True, True).then_inc(pe, 1)
-        g.tensor.matmul(ps[64:128, 0:e], blk, T.xa[:, w:w + e], True, True).then_inc(pe, 1)
-        g.vector.wait_ge(pe, 2)
-        g.vector.tensor_copy(T["es%d" % i][:, 0:e], ps[:, 0:e]).then_inc(S["ec%d" % i], 1)
-        g.wait_ge(S["ec%d" % i], 1)
-        send(cores[r], T["el%d" % rank][:, 0:e], T["es%d" % i][:, 0:e], S["ea%d" % rank])
+    swapped = _count(topo.mask(partner, core))
+    have = []
+    for (kind, d, lo, hi) in prog:
+        xs = T.xb if kind == "C2" else T.xa
+        wants = []
+        if max(P * d + P, hi) > CUT:
+            wants.append(("xrr", swapped) if kind == "C2" else ("ldr", 16))
+        if min(P * d, lo) < CUT:
+            wants.append(("xrl", swapped) if kind == "C2" else ("ldl", 16))
+        for (name, cnt) in wants:
+            if name not in have:
+                g.tensor.wait_ge(S[name], cnt)
+                have.append(name)
+        b = bank[(d, lo, hi)]
+        ins = g.tensor.matmul(T["ps%d" % b][:, 0:hi - lo], xs[:, P * d:P * d + P], xs[:, lo:hi],
+                              kind != "C2", kind != "C1")
+        if kind != "C1":
+            ins.then_inc(S["pe%d" % b], 1)
 
-    if rank > 0:
-        g.vector.memset(T.lz[:, CB:2 * CB], 0.0).then_inc(S.lzs, 1)
-        g.vector.wait_ge(S.ld, 16)
-        g.vector.tensor_copy(T.lz[:, 0:CB], T.xa[:, CB * rank:CB * rank + CB]).then_inc(S.lzs, 1)
-
-    def job_pass(xs, first):
-        for d in jobs:
-            for (b, lo, hi) in seg[d]:
-                ins = g.tensor.matmul(T["ps%d" % b][:, 0:hi - lo], xs[:, P * d:P * d + P], xs[:, lo:hi],
-                                      first, not first)
-                if not first:
-                    ins.then_inc(S["pe%d" % b], 1)
-
-    def own_pass(xs, first):
-        ps = T["ps%d" % own_bank]
-        w = w_own
-        blk = xs[:, CB * rank:CB * rank + CB]
-        if first:
-            g.tensor.matmul(ps[:, 0:w], T.lz[:, :], xs[:, 0:w], True, False)
-            g.tensor.matmul(ps[64:128, 0:w], blk, xs[:, w:2 * w], False, False)
-        else:
-            g.tensor.matmul(ps[0:64, 0:w], blk, xs[:, 0:w], False, True).then_inc(S["pe%d" % own_bank], 1)
-            g.tensor.matmul(ps[64:128, 0:w], blk, xs[:, w:2 * w], False, True).then_inc(S["pe%d" % own_bank], 1)
-
-    job_pass(T.xa, True)
-    if rank > 0:
-        g.tensor.wait_ge(S.lzs, 2)
-        own_pass(T.xa, True)
-    g.tensor.wait_ge(S.xr, _count(topo.mask(partner, core)))
-    job_pass(T.xb, False)
-    if rank > 0:
-        own_pass(T.xb, False)
-
-    n = 0
     seen = []
-    for d in jobs:
-        for r in (2 * d + 1, 2 * d):
-            if r == 0:
+
+    def relay(dst, r, unit, sem):
+        d, lo, hi = unit
+        p0 = CB * (r - 2 * d)
+        cnt = 0
+        for (c0, c1, off, wp) in _parts(r):
+            if c0 >= hi or c1 <= lo:
                 continue
-            e0 = EARLY.get(r, 0)
-            w = 32 * r
-            p0 = CB * (r - 2 * d)
-            st = T["stage%d" % n]
-            cnt = 0
             for h in (0, 1):
-                for (b, lo, hi) in seg[d]:
-                    a = max(lo, h * w + e0)
-                    e = min(hi, (h + 1) * w)
+                for (b, slo, shi) in seg[unit]:
+                    a = max(slo, c0 + h * wp)
+                    e = min(shi, c0 + (h + 1) * wp)
                     if a >= e:
                         continue
                     if b not in seen:
                         g.vector.wait_ge(S["pe%d" % b], 1)
                         seen.append(b)
-                    g.vector.tensor_copy(st[CB * h:CB * h + CB, a - h * w:e - h * w],
-                                         T["ps%d" % b][p0:p0 + CB, a - lo:e - lo]).then_inc(S["cp%d" % n], 1)
+                    la = off + a - c0 - h * wp
+                    g.vector.tensor_copy(dst[CB * h:CB * h + CB, la:la + e - a],
+                                         T["ps%d" % b][p0:p0 + CB, a - slo:e - slo]).then_inc(sem, 1)
                     cnt += 1
+        return cnt
+
+    mine = sends_of(core)
+    nad = 0
+    n = 0
+    for (unit, _c) in _finished(me, prog):
+        for (r, u, a, b, sem, _col) in mine:
+            if u != unit:
+                continue
+            st = T["stage%d" % n]
+            cnt = relay(st, r, unit, S["cp%d" % n])
             g.wait_ge(S["cp%d" % n], cnt)
-            send(cores[r], T["land%d" % me][:, e0:w], st[:, e0:w], S["ar%d" % me])
+            send(cores[r], T["land%d" % rank][:, a:b], st[:, a:b], S[sem], tile_mask(core, cores[r]))
             n += 1
+        if unit[0] == me and rank > 0:
+            nad += relay(acc, rank, unit, S.ad)
 
     if rank > 0:
-        w = w_own
-        e0 = EARLY.get(rank, 0)
-        ps = T["ps%d" % own_bank]
-        g.vector.wait_ge(S["pe%d" % own_bank], 2)
-        parts = []
-        if e0:
-            parts.append((0, e0, [(T["el%d" % q], S["ea%d" % q], _count(topo.mask(cores[q], core)))
-                                  for q in range(N) if chip_index(cores[q]) != me]))
-        srcs = [k for k in range(NCH) if k != me]
-        srcs.sort(key=lambda k: units_before(k, rank))
-        parts.append((e0, w, [(T["land%d" % k], S["ar%d" % k], _count(topo.mask(sender(k, me), core)))
-                              for k in srcs]))
-        nad = 0
-        for (a, b, lands) in parts:
-            for j, (buf, sem, cnt) in enumerate(lands):
-                g.vector.wait_ge(sem, cnt)
-                if nad:
-                    g.vector.wait_ge(S.ad, nad)
-                if j == len(lands) - 1:
-                    g.vector.tensor_tensor(T.res[:, a:b], ps[:, a:b], buf[:, a:b], AluOpType.add).then_inc(S.fin, 1)
-                else:
-                    g.vector.tensor_tensor(ps[:, a:b], ps[:, a:b], buf[:, a:b], AluOpType.add).then_inc(S.ad, 1)
-                    nad += 1
-        g.sync.wait_ge(S.fin, len(parts))
-        g.scalar.wait_ge(S.fin, len(parts))
-        g.sync.dma_start(T.y[:, 0:w], T.res[0:64, 0:w]).then_inc(S.st, 16)
-        g.scalar.dma_start(T.y[:, w:2 * w], T.res[64:128, 0:w]).then_inc(S.st, 16)
-        g.wait_ge(S.st, 32)
+        parts = _parts(rank)
+        lands = []
+        for q in range(N):
+            if q == rank:
+                continue
+            for (r, _u, a, b, sem, col) in sends_of(cores[q]):
+                if r == rank:
+                    lands.append((a, col, q, b, sem))
+        whole = [x for x in lands if len(parts) > 1 and (x[0], x[3]) == (0, 32 * rank)]
+        order = sorted(whole, key=lambda x: x[1])
+        for (_c0, _c1, off, wp) in parts:
+            order += sorted([x for x in lands if x not in whole and x[0] == off], key=lambda x: x[1])
+        for i, (a, _col, q, b, sem) in enumerate(order):
+            last = not [x for x in order[i + 1:] if x[0] < b and x[3] > a]
+            g.vector.wait_ge(S[sem], _count(tile_mask(cores[q], core)))
+            g.vector.wait_ge(S.ad, nad)
+            buf = T["land%d" % q]
+            if last:
+                pi = [j for j, pt in enumerate(parts) if pt[2] == a][0]
+                g.vector.tensor_tensor(T.res[:, a:b], acc[:, a:b], buf[:, a:b], AluOpType.add).then_inc(
+                    S["fin%d" % pi], 1)
+            else:
+                g.vector.tensor_tensor(acc[:, a:b], acc[:, a:b], buf[:, a:b], AluOpType.add).then_inc(S.ad, 1)
+                nad += 1
+        for i, (c0, c1, off, wp) in enumerate(parts):
+            g.sync.wait_ge(S["fin%d" % i], 1)
+            g.scalar.wait_ge(S["fin%d" % i], 1)
+            g.sync.dma_start(T.y[:, c0:c0 + wp], T.res[0:64, off:off + wp]).then_inc(S.st, 16)
+            g.scalar.dma_start(T.y[:, c0 + wp:c1], T.res[64:128, off:off + wp]).then_inc(S.st, 16)
+        g.wait_ge(S.st, 32 * len(parts))
     g.wait_ge(S.snt, sent[0])

from concourse.mybir import AluOpType

N = 10
CB = 64
P = 128
NCH = 5
TOP = NCH - 1
WMAX = 32 * (N - 1)
EC = 128
CUT = 320
NSEND = 8
NBANK = 8

JOBS = {
    0: ((4, 1), (3, 2)),
    1: ((3, 2), (4, 0)),
    2: ((4, 0), (3, 1)),
    3: ((2, 1, 0), (4,)),
    4: ((3, 0), (2, 1)),
}
OWN_LAST = ((1, 0),)


def _w(d):
    return P * d + CB


def _unit(k, d, lo, hi):
    if d == TOP and k != TOP:
        return (TOP, 0, EC) if hi <= EC else (TOP, EC, _w(TOP))
    return (d, 0, _w(d))


def _segs(k, d):
    lo = EC if (d == TOP and k != TOP) else 0
    if P * d >= CUT and _w(d) > CUT:
        return [(d, CUT, _w(d)), (d, lo, CUT)]
    return [(d, lo, _w(d))]


def _plan(k, side):
    jobs = JOBS[k][side]
    first = _segs(k, jobs[0])
    own = _segs(k, k)
    ahead, rest = [], []
    if k == TOP:
        ahead += [("R",) + own[0]]
        rest += [("R",) + s for s in own[1:]]
        own = []
    if len(first) > 1:
        ahead += [("C1",) + first[0]]
        rest += [("C1",) + first[1]]
    else:
        rest += [("C1",) + first[0]]
    prog = list(ahead)
    if k != TOP:
        prog += [("R", TOP, 0, EC)]
    prog += rest
    if (k, side) not in OWN_LAST:
        prog += [("R",) + s for s in own]
    for d in jobs[1:]:
        prog += [("C1",) + s for s in _segs(k, d)]
    for d in jobs:
        prog += [("C2",) + s for s in _segs(k, d)]
    if (k, side) in OWN_LAST:
        prog += [("R",) + s for s in own]
    return prog


def _parts(r):
    w = CB * r
    if r // 2 == TOP:
        return [(0, EC, 0, EC // 2), (EC, w, EC // 2, (w - EC) // 2)]
    return [(0, w, 0, w // 2)]


def _lrange(r, unit):
    _d, lo, hi = unit
    sel = [(off, off + wp) for (c0, c1, off, wp) in _parts(r) if c0 < hi and c1 > lo]
    return min(a for a, _b in sel), max(b for _a, b in sel)


def _finished(k, prog):
    left = {}
    for (kind, d, lo, hi) in prog:
        if kind != "C1":
            u = _unit(k, d, lo, hi)
            left[u] = left.get(u, 0) + 1
    out = []
    col = 0
    for (kind, d, lo, hi) in prog:
        col += hi - lo
        if kind != "C1":
            u = _unit(k, d, lo, hi)
            left[u] -= 1
            if left[u] == 0:
                out.append((u, col))
    return out


SCRATCH = {
    "xa": ("sbuf", [P, N * CB], "float32"),
    "xb": ("sbuf", [P, N * CB], "float32"),
    "res": ("sbuf", [P, WMAX], "float32"),
}
for _k in range(N):
    SCRATCH["land%d" % _k] = ("sbuf", [P, WMAX], "float32")
for _k in range(NSEND):
    SCRATCH["stage%d" % _k] = ("sbuf", [P, WMAX], "float32")
for _k in range(NBANK):
    SCRATCH["ps%d" % _k] = ("psum", [P, 512], "float32")

SEMAPHORES = (["ldr", "ldl", "xrr", "xrl", "snt", "ad", "fin0", "fin1", "st"]
              + ["pe%d" % i for i in range(NBANK)]
              + ["ar%d" % i for i in range(N)]
              + ["ea%d" % i for i in range(N)]
              + ["cp%d" % i for i in range(NSEND)])


def _count(mask):
    return bin(mask).count("1")


def rank_program(g, core, T, topo):
    rank = T.rank_of(core)
    if rank is None:
        return
    S = T.sem
    cores = list(T.cores)
    chips = []
    for c in cores:
        if topo.chip(c) not in chips:
            chips.append(topo.chip(c))

    def chip_index(c):
        return chips.index(topo.chip(c))

    def side_of(c):
        return 0 if topo.die(c) == topo.die(cores[0]) else 1

    def member(k, side):
        return [c for c in cores if chip_index(c) == k and side_of(c) == side][0]

    def tile_mask(src, dst):
        m = topo.mask(src, dst)
        if topo.chip(src) != topo.chip(dst):
            return m
        far = [c for c in cores if topo.chip(c) != topo.chip(src)][0]
        rest = m & ~topo.mask(src, far)
        return rest if rest and P % _count(rest) == 0 else m

    def sends_of(c):
        rq = T.rank_of(c)
        k = chip_index(c)
        out = []
        for (u, col) in _finished(k, _plan(k, side_of(c))):
            d = u[0]
            for r in (2 * d + 1, 2 * d):
                if r == 0 or r == rq:
                    continue
                a, b = _lrange(r, u)
                out.append((r, u, a, b, ("ea%d" if u == (TOP, 0, EC) else "ar%d") % rq, col))
        return out

    me = chip_index(core)
    partner = member(me, 1 - side_of(core))
    prog = _plan(me, side_of(core))
    sent = [0]

    def send(dst, out_ap, in_ap, sem, m):
        rid, pid, _se = topo.addr(dst)
        g.remote_dma(out_ap=out_ap, in_ap=in_ap, remote_sem=sem, local_sem=S.snt, pid=pid, routing_id=rid,
                     dma_engine_mask=m)
        sent[0] += _count(m)

    nb = 0
    bank = {}
    seg = {}
    for (_kind, d, lo, hi) in prog:
        if (d, lo, hi) in bank:
            continue
        bank[(d, lo, hi)] = nb
        seg.setdefault(_unit(me, d, lo, hi), []).append((nb, lo, hi))
        nb += 1
    acc = T["ps%d" % nb]

    g.sync.dma_start(T.xa[:, CUT:N * CB], T.x[:, CUT:N * CB]).then_inc(S.ldr, 16)
    g.sync.dma_start(T.xa[:, 0:CUT], T.x[:, 0:CUT]).then_inc(S.ldl, 16)

    need = max(max(P * d + P, hi) for (kind, d, lo, hi) in _plan(me, 1 - side_of(core)) if kind == "C2")
    g.wait_ge(S.ldr, 16)
    send(partner, T.xb[:, CUT:need], T.xa[:, CUT:need], S.xrr, topo.mask(core, partner))
    g.wait_ge(S.ldl, 16)
    send(partner, T.xb[:, 0:CUT], T.xa[:, 0:CUT], S.xrl, topo.mask(core, partner))

    swapped = _count(topo.mask(partner, core))
    have = []
    for (kind, d, lo, hi) in prog:
        xs = T.xb if kind == "C2" else T.xa
        wants = []
        if max(P * d + P, hi) > CUT:
            wants.append(("xrr", swapped) if kind == "C2" else ("ldr", 16))
        if min(P * d, lo) < CUT:
            wants.append(("xrl", swapped) if kind == "C2" else ("ldl", 16))
        for (name, cnt) in wants:
            if name not in have:
                g.tensor.wait_ge(S[name], cnt)
                have.append(name)
        b = bank[(d, lo, hi)]
        ins = g.tensor.matmul(T["ps%d" % b][:, 0:hi - lo], xs[:, P * d:P * d + P], xs[:, lo:hi],
                              kind != "C2", kind != "C1")
        if kind != "C1":
            ins.then_inc(S["pe%d" % b], 1)

    seen = []

    def relay(dst, r, unit, sem):
        d, lo, hi = unit
        p0 = CB * (r - 2 * d)
        cnt = 0
        for (c0, c1, off, wp) in _parts(r):
            if c0 >= hi or c1 <= lo:
                continue
            for h in (0, 1):
                for (b, slo, shi) in seg[unit]:
                    a = max(slo, c0 + h * wp)
                    e = min(shi, c0 + (h + 1) * wp)
                    if a >= e:
                        continue
                    if b not in seen:
                        g.vector.wait_ge(S["pe%d" % b], 1)
                        seen.append(b)
                    la = off + a - c0 - h * wp
                    g.vector.tensor_copy(dst[CB * h:CB * h + CB, la:la + e - a],
                                         T["ps%d" % b][p0:p0 + CB, a - slo:e - slo]).then_inc(sem, 1)
                    cnt += 1
        return cnt

    mine = sends_of(core)
    nad = 0
    n = 0
    for (unit, _c) in _finished(me, prog):
        for (r, u, a, b, sem, _col) in mine:
            if u != unit:
                continue
            st = T["stage%d" % n]
            cnt = relay(st, r, unit, S["cp%d" % n])
            g.wait_ge(S["cp%d" % n], cnt)
            send(cores[r], T["land%d" % rank][:, a:b], st[:, a:b], S[sem], tile_mask(core, cores[r]))
            n += 1
        if unit[0] == me and rank > 0:
            nad += relay(acc, rank, unit, S.ad)

    if rank > 0:
        parts = _parts(rank)
        lands = []
        for q in range(N):
            if q == rank:
                continue
            for (r, _u, a, b, sem, col) in sends_of(cores[q]):
                if r == rank:
                    lands.append((a, col, q, b, sem))
        whole = [x for x in lands if len(parts) > 1 and (x[0], x[3]) == (0, 32 * rank)]
        order = sorted(whole, key=lambda x: x[1])
        for (_c0, _c1, off, wp) in parts:
            order += sorted([x for x in lands if x not in whole and x[0] == off], key=lambda x: x[1])
        for i, (a, _col, q, b, sem) in enumerate(order):
            last = not [x for x in order[i + 1:] if x[0] < b and x[3] > a]
            g.vector.wait_ge(S[sem], _count(tile_mask(cores[q], core)))
            g.vector.wait_ge(S.ad, nad)
            buf = T["land%d" % q]
            if last:
                pi = [j for j, pt in enumerate(parts) if pt[2] == a][0]
                g.vector.tensor_tensor(T.res[:, a:b], acc[:, a:b], buf[:, a:b], AluOpType.add).then_inc(
                    S["fin%d" % pi], 1)
            else:
                g.vector.tensor_tensor(acc[:, a:b], acc[:, a:b], buf[:, a:b], AluOpType.add).then_inc(S.ad, 1)
                nad += 1
        for i, (c0, c1, off, wp) in enumerate(parts):
            g.sync.wait_ge(S["fin%d" % i], 1)
            g.scalar.wait_ge(S["fin%d" % i], 1)
            g.sync.dma_start(T.y[:, c0:c0 + wp], T.res[0:64, off:off + wp]).then_inc(S.st, 16)
            g.scalar.dma_start(T.y[:, c0 + wp:c1], T.res[64:128, off:off + wp]).then_inc(S.st, 16)
        g.wait_ge(S.st, 32 * len(parts))
    g.wait_ge(S.snt, sent[0])
